import numpy as np, ml_dtypes
CORES = [7,15,23,39,47,63,71,79,87,95,119,127]
N = 12
KB, QP, ROOT = 2, 256, 10
def setup_inputs(rng):
    return {"q": rng.standard_normal((N, 128, QP), dtype=np.float32).astype(ml_dtypes.bfloat16), "k": rng.standard_normal((N, 128, KB * 128), dtype=np.float32).astype(ml_dtypes.bfloat16), "v": rng.standard_normal((N, 128, KB * 128), dtype=np.float32).astype(ml_dtypes.bfloat16)}
def setup_inputs_big(rng):
    d = setup_inputs(rng)
    for k in ("q", "k", "v"): d[k] = (d[k].astype(np.float32) * 1024.0).astype(d[k].dtype)
    return d
def setup_inputs_small(rng):
    d = setup_inputs(rng)
    for k in ("q", "k", "v"): d[k] = (d[k].astype(np.float32) * (1 / 1024.0)).astype(d[k].dtype)
    return d
def setup_inputs_apart(rng):
    d = setup_inputs(rng)
    f = (10.0 ** rng.permutation(np.linspace(-1.5, 1.5, N))).astype(np.float32).reshape(N, 1, 1)
    for k in ("q", "k", "v"): d[k] = (d[k].astype(np.float32) * f).astype(d[k].dtype)
    return d
def reference(q, k, v):
    Q, K, V = q.astype(np.float64), k.astype(np.float64), v.astype(np.float64)
    o = np.zeros((128, QP))
    for j in range(N):
        for b in range(KB):
            o += V[j][:, 128 * b:128 * b + 128].T @ np.maximum(K[j][:, 128 * b:128 * b + 128].T @ Q[ROOT], 0.0)
    y = np.full((N, 128, QP), np.nan)
    y[ROOT] = o
    return {"y": y.astype(ml_dtypes.bfloat16 if q.dtype != np.float64 else np.float64)}

@@ -1,0 +1,212 @@
+import numpy as np
+from concourse.bass import DstId, RemoteDMATransfer
+from concourse.mybir import AluOpType
+
+NR = 12
+QP = 256
+KB = 2
+BW = 128
+KW = KB * BW
+SLOT = 2 * KW
+NBANK = 6
+MOVE = 2
+PAIRS = 0
+SPLIT = True
+LOOK = 2
+NE_KV = 8
+NE_Q = 8
+NE_O = 8
+
+SCRATCH = {
+    "qs": ("sbuf", [128, QP], "bfloat16"),
+    "kv": ("sbuf", [128, NR * SLOT], "bfloat16"),
+    "s": ("sbuf", [128, NR * KB * QP], "bfloat16"),
+    "zero": ("sbuf", [128, QP], "float32"),
+    "osend": ("sbuf", [128, QP], "bfloat16"),
+    "oin": ("sbuf", [128, NR * QP], "bfloat16"),
+    "acc0": ("sbuf", [128, QP], "float32"),
+    "acc1": ("sbuf", [128, QP], "float32"),
+    "ysb": ("sbuf", [128, QP], "bfloat16"),
+    "po": ("psum", [128, 512], "float32"),
+}
+for _i in range(NBANK):
+    SCRATCH["ps%d" % _i] = ("psum", [128, 512], "float32")
+
+SEMAPHORES = ["qa", "z", "od", "oc", "yr", "ys", "snt"]
+for _r in range(NR):
+    SEMAPHORES += ["ka%d" % _r, "va%d" % _r, "oa%d" % _r, "ac%d" % _r]
+    for _b in range(KB):
+        SEMAPHORES += ["sd%d_%d" % (_r, _b), "rd%d_%d" % (_r, _b)]
+
+
+def engines(mask, n):
+    out, left = 0, n
+    for b in range(16):
+        if left and (mask >> b) & 1:
+            out |= 1 << b
+            left -= 1
+    return out
+
+
+def make_plan(T, topo):
+    cores = list(T.cores)
+    root = cores[T.root]
+    chips = [topo.chip(c) for c in cores]
+    second = None
+    for c in cores:
+        if topo.mates(topo.chip(c), topo.chip(root)) and topo.may_write(c, root) and topo.may_write(root, c):
+            second = c
+    site = {}
+    for r, c in enumerate(cores):
+        site[r] = root
+        if second is not None and c != second and topo.same_plane(topo.chip(c), topo.chip(second)):
+            site[r] = second
+    cand = [r for r in range(len(cores)) if site[r] != root and topo.may_write(cores[r], root)]
+    cand.sort(key=lambda r: sum(1 for ch in chips if topo.mates(ch, chips[r])))
+    for r in cand[:MOVE]:
+        site[r] = root
+
+    pairs = []
+    for r, c in enumerate(cores):
+        if len(pairs) < PAIRS and c != root and topo.same_plane(chips[r], topo.chip(root)):
+            for m, d in enumerate(cores):
+                if topo.mates(chips[m], chips[r]) and topo.may_write(d, c) and site[m] != root:
+                    site[r], site[m] = c, c
+                    pairs.append(c)
+
+    def hops(r, s):
+        a, b = chips[r], topo.chip(s)
+        if cores[r] == s:
+            return 0
+        if a == b or topo.mates(a, b):
+            return 1
+        return 2 if topo.same_plane(a, b) else 3
+
+    order = {}
+    for s in [root] + pairs + ([second] if second is not None else []):
+        mine = sorted([r for r in site if site[r] == s], key=lambda r: (hops(r, s), r))
+        if mine:
+            order[s] = mine
+    return root, site, order
+
+
+def rank_program(g, core, T, topo):
+    rank = T.rank_of(core)
+    if rank is None:
+        return
+    root, site, order = make_plan(T, topo)
+    cores = list(T.cores)
+    sem = T.sem
+    pe, ve = g.tensor, g.vector
+    sent = 0
+
+    def kcols(r):
+        return T.kv[:, r * SLOT:r * SLOT + KW]
+
+    def vcols(r):
+        return T.kv[:, r * SLOT + KW:(r + 1) * SLOT]
+
+    def write(dst, out_ap, in_ap, rsem, n):
+        rid, pid, _ = topo.addr(dst)
+        g.remote_dma(out_ap=out_ap, in_ap=in_ap, remote_sem=rsem, local_sem=sem.snt, pid=pid, routing_id=rid,
+                     dma_engine_mask=engines(topo.mask(core, dst), n))
+        return n
+
+    ka, va = sem["ka%d" % rank], sem["va%d" % rank]
+    if core == root:
+        g.sync.dma_start(T.qs[:, :], T.q[:, :]).then_inc(sem.qa, 16)
+        g.scalar.dma_start(kcols(rank), T.k[:, :]).then_inc(ka, 16)
+        g.sync.dma_start(vcols(rank), T.v[:, :]).then_inc(va, 16)
+    else:
+        g.sync.dma_start(kcols(rank), T.k[:, :]).then_inc(ka, 16)
+        g.scalar.dma_start(vcols(rank), T.v[:, :]).then_inc(va, 16)
+
+    if core == root:
+        g.wait_ge(sem.qa, 16)
+        dsts = [s for s in order if s != root]
+        if len(dsts) == 1:
+            sent += write(dsts[0], T.qs[:, :], T.qs[:, :], sem.qa, NE_Q)
+        elif dsts:
+            mask = topo.mask(core, dsts[0])
+            for s in dsts:
+                mask &= topo.mask(core, s)
+            g.remote_dma_fused([RemoteDMATransfer(dst_ids=[DstId(rid=topo.addr(s)[0], pnc=topo.addr(s)[1]) for s in dsts],
+                                                  dma_engine_mask=engines(mask, NE_Q), remote_sem=sem.qa,
+                                                  srcs=[T.qs[:, :]], dsts=[T.qs[:, :] for s in dsts])], local_sem=sem.snt)
+            sent += NE_Q
+    if site[rank] != core:
+        g.wait_ge(ka, 16)
+        if SPLIT:
+            sent += write(site[rank], kcols(rank), kcols(rank), ka, NE_KV)
+            g.wait_ge(va, 16)
+            sent += write(site[rank], vcols(rank), vcols(rank), va, NE_KV)
+        else:
+            g.wait_ge(va, 16)
+            slot = T.kv[:, rank * SLOT:(rank + 1) * SLOT]
+            sent += write(site[rank], slot, slot, ka, NE_KV)
+
+    if core in order:
+        blocks = [(r, b) for r in order[core] for b in range(KB)]
+        nb = len(blocks)
+        ve.memset(T.zero[:, :], 0.0).then_inc(sem.z, 1)
+        ve.wait_ge(sem.z, 1)
+        pe.wait_ge(sem.qa, 16 if core == root else NE_Q)
+        seen = set()
+
+        def arrived(name, r):
+            if cores[r] != core and not SPLIT:
+                name = "ka"
+            if (name, r) not in seen:
+                seen.add((name, r))
+                pe.wait_ge(sem["%s%d" % (name, r)], 16 if cores[r] == core else NE_KV)
+
+        def s_stage(i):
+            r, b = blocks[i]
+            arrived("ka", r)
+            bank = T["ps%d" % (i % NBANK)]
+            pe.matmul(out=bank[:, 0:QP], lhsT=T.kv[:, r * SLOT + b * BW:r * SLOT + (b + 1) * BW], rhs=T.qs[:, :],
+                      start=True, stop=True).then_inc(sem["sd%d_%d" % (r, b)], 1)
+            ve.wait_ge(sem["sd%d_%d" % (r, b)], 1)
+            ve.tensor_tensor(out=T.s[:, (r * KB + b) * QP:(r * KB + b + 1) * QP], in0=bank[:, 0:QP], in1=T.zero[:, :],
+                             op=AluOpType.max).then_inc(sem["rd%d_%d" % (r, b)], 1)
+
+        def o_stage(i):
+            r, b = blocks[i]
+            arrived("va", r)
+            pe.wait_ge(sem["rd%d_%d" % (r, b)], 1)
+            pe.matmul(out=T.po[:, 0:QP], lhsT=T.kv[:, r * SLOT + KW + b * BW:r * SLOT + KW + (b + 1) * BW],
+                      rhs=T.s[:, (r * KB + b) * QP:(r * KB + b + 1) * QP],
+                      start=(i == 0), stop=(i == nb - 1)).then_inc(sem.od, 1)
+
+        for i in range(nb + LOOK):
+            if i < nb:
+                s_stage(i)
+            if i >= LOOK:
+                o_stage(i - LOOK)
+
+        if core != root:
+            ve.wait_ge(sem.od, nb)
+            ve.tensor_copy(out=T.osend[:, :], in_=T.po[:, 0:QP]).then_inc(sem.oc, 1)
+            g.wait_ge(sem.oc, 1)
+            sent += write(root, T.oin[:, rank * QP:(rank + 1) * QP], T.osend[:, :], sem["oa%d" % rank], NE_O)
+        else:
+            others = [T.rank_of(s) for s in order if s != root]
+            ve.wait_ge(sem.od, nb)
+            cur = T.po[:, 0:QP]
+            if not others:
+                ve.tensor_copy(out=T.ysb[:, :], in_=cur).then_inc(sem.yr, 1)
+            for j, r in enumerate(others):
+                last = j == len(others) - 1
+                ve.wait_ge(sem["oa%d" % r], NE_O)
+                out = T.ysb[:, :] if last else T["acc%d" % (j % 2)][:, :]
+                ve.tensor_tensor(out=out, in0=cur, in1=T.oin[:, r * QP:(r + 1) * QP],
+                                 op=AluOpType.add).then_inc(sem.yr if last else sem["ac%d" % r], 1)
+                if not last:
+                    ve.wait_ge(sem["ac%d" % r], 1)
+                cur = out
+            g.sync.wait_ge(sem.yr, 1)
+            g.sync.dma_start(T.y[:, :], T.ysb[:, :]).then_inc(sem.ys, 16)
+            g.sync.wait_ge(sem.ys, 16)
+
+    if sent:
+        g.wait_ge(sem.snt, sent)

@@ -9,7 +9,7 @@ BW = 128
 KW = KB * BW
 SLOT = 2 * KW
 NBANK = 6
-MOVE = 2
+MOVE = 1
 PAIRS = 0
 SPLIT = True
 LOOK = 2

@@ -3,17 +3,21 @@ from concourse.bass import DstId, RemoteDMATransfer
 from concourse.mybir import AluOpType
 
 NR = 12
+NCORES = 128
 QP = 256
+HQ = QP // 2
 KB = 2
 BW = 128
 KW = KB * BW
 SLOT = 2 * KW
 NBANK = 6
 MOVE = 1
-PAIRS = 0
-SPLIT = True
+PAIRS = 1
+VIA_ROOT = 2
+VIA_SECOND = 1
 LOOK = 2
 NE_KV = 8
+NE_ON = 8
 NE_Q = 8
 NE_O = 8
 
@@ -52,27 +56,39 @@ def make_plan(T, topo):
     cores = list(T.cores)
     root = cores[T.root]
     chips = [topo.chip(c) for c in cores]
+    rchip = topo.chip(root)
     second = None
     for c in cores:
-        if topo.mates(topo.chip(c), topo.chip(root)) and topo.may_write(c, root) and topo.may_write(root, c):
+        if topo.mates(topo.chip(c), rchip) and topo.may_write(c, root) and topo.may_write(root, c):
             second = c
-    site = {}
+    dest, via, work, groups = {}, {}, {}, []
     for r, c in enumerate(cores):
-        site[r] = root
-        if second is not None and c != second and topo.same_plane(topo.chip(c), topo.chip(second)):
-            site[r] = second
-    cand = [r for r in range(len(cores)) if site[r] != root and topo.may_write(cores[r], root)]
-    cand.sort(key=lambda r: sum(1 for ch in chips if topo.mates(ch, chips[r])))
-    for r in cand[:MOVE]:
-        site[r] = root
-
-    pairs = []
-    for r, c in enumerate(cores):
-        if len(pairs) < PAIRS and c != root and topo.same_plane(chips[r], topo.chip(root)):
+        if len(groups) < PAIRS and c != root and topo.same_plane(chips[r], rchip):
             for m, d in enumerate(cores):
-                if topo.mates(chips[m], chips[r]) and topo.may_write(d, c) and site[m] != root:
-                    site[r], site[m] = c, c
-                    pairs.append(c)
+                if topo.mates(chips[m], chips[r]) and topo.may_write(d, c) and topo.may_write(c, d) \
+                        and topo.may_write(d, root) and topo.may_write(root, d):
+                    dest[r], dest[m] = d, c
+                    work[c], work[d] = ([r, m], 0, HQ), ([m, r], HQ, QP)
+                    groups.append([(r, 0, HQ), (m, HQ, QP)])
+    rest = [r for r in range(len(cores)) if r not in dest]
+    far = [r for r in rest if second is not None and cores[r] != second and topo.same_plane(chips[r], topo.chip(second))]
+    far.sort(key=lambda r: sum(1 for ch in chips if topo.mates(ch, chips[r])))
+    far = far[MOVE:]
+    for r in rest:
+        dest[r] = second if r in far else (root if cores[r] != root else None)
+
+    def relay(r):
+        for x in range(NCORES):
+            if topo.chip(x) == chips[r] and topo.die(x) != topo.die(cores[r]) and T.rank_of(x) is None \
+                    and topo.may_write(x, dest[r]):
+                return x
+        return None
+
+    for site, n in ((root, VIA_ROOT), (second, VIA_SECOND)):
+        same = [r for r in rest if dest[r] == site and site is not None and topo.same_plane(chips[r], topo.chip(site))]
+        for r in (sorted(same)[-n:] if n else []):
+            if relay(r) is not None:
+                via[r] = relay(r)
 
     def hops(r, s):
         a, b = chips[r], topo.chip(s)
@@ -80,21 +96,18 @@ def make_plan(T, topo):
             return 0
         if a == b or topo.mates(a, b):
             return 1
-        return 2 if topo.same_plane(a, b) else 3
+        return (2 if topo.same_plane(a, b) else 3) + (2 if r in via else 0)
 
-    order = {}
-    for s in [root] + pairs + ([second] if second is not None else []):
-        mine = sorted([r for r in site if site[r] == s], key=lambda r: (hops(r, s), r))
-        if mine:
-            order[s] = mine
-    return root, site, order
+    work[root] = (sorted([r for r in rest if r not in far], key=lambda r: (hops(r, root), r)), 0, QP)
+    if far:
+        work[second] = (sorted(far, key=lambda r: (hops(r, second), r)), 0, QP)
+        groups.append([(cores.index(second), 0, QP)])
+    return root, dest, via, work, groups
 
 
 def rank_program(g, core, T, topo):
     rank = T.rank_of(core)
-    if rank is None:
-        return
-    root, site, order = make_plan(T, topo)
+    root, dest, via, work, groups = make_plan(T, topo)
     cores = list(T.cores)
     sem = T.sem
     pe, ve = g.tensor, g.vector
@@ -112,6 +125,16 @@ def rank_program(g, core, T, topo):
                      dma_engine_mask=engines(topo.mask(core, dst), n))
         return n
 
+    if rank is None:
+        for r in via:
+            if via[r] == core:
+                g.wait_ge(sem["ka%d" % r], NE_ON)
+                sent += write(dest[r], kcols(r), kcols(r), sem["ka%d" % r], NE_KV)
+                g.wait_ge(sem["va%d" % r], NE_ON)
+                sent += write(dest[r], vcols(r), vcols(r), sem["va%d" % r], NE_KV)
+                g.wait_ge(sem.snt, sent)
+        return
+
     ka, va = sem["ka%d" % rank], sem["va%d" % rank]
     if core == root:
         g.sync.dma_start(T.qs[:, :], T.q[:, :]).then_inc(sem.qa, 16)
@@ -123,39 +146,44 @@ def rank_program(g, core, T, topo):
 
     if core == root:
         g.wait_ge(sem.qa, 16)
-        dsts = [s for s in order if s != root]
-        if len(dsts) == 1:
-            sent += write(dsts[0], T.qs[:, :], T.qs[:, :], sem.qa, NE_Q)
-        elif dsts:
-            mask = topo.mask(core, dsts[0])
-            for s in dsts:
-                mask &= topo.mask(core, s)
-            g.remote_dma_fused([RemoteDMATransfer(dst_ids=[DstId(rid=topo.addr(s)[0], pnc=topo.addr(s)[1]) for s in dsts],
-                                                  dma_engine_mask=engines(mask, NE_Q), remote_sem=sem.qa,
-                                                  srcs=[T.qs[:, :]], dsts=[T.qs[:, :] for s in dsts])], local_sem=sem.snt)
-            sent += NE_Q
-    if site[rank] != core:
-        g.wait_ge(ka, 16)
-        if SPLIT:
-            sent += write(site[rank], kcols(rank), kcols(rank), ka, NE_KV)
-            g.wait_ge(va, 16)
-            sent += write(site[rank], vcols(rank), vcols(rank), va, NE_KV)
-        else:
-            g.wait_ge(va, 16)
-            slot = T.kv[:, rank * SLOT:(rank + 1) * SLOT]
-            sent += write(site[rank], slot, slot, ka, NE_KV)
+        transfers, used = [], 0
+        for c0 in (0, HQ):
+            dsts = [cores[r] for grp in groups for (r, a, b) in grp if a == c0 and b - a == HQ]
+            if dsts:
+                mask = topo.mask(core, dsts[0])
+                for s in dsts:
+                    mask &= topo.mask(core, s)
+                mine = engines(mask & ~used, NE_Q // 2)
+                used |= mine
+                transfers.append(RemoteDMATransfer(
+                    dst_ids=[DstId(rid=topo.addr(s)[0], pnc=topo.addr(s)[1]) for s in dsts], dma_engine_mask=mine,
+                    remote_sem=sem.qa, srcs=[T.qs[:, c0:c0 + HQ]], dsts=[T.qs[:, c0:c0 + HQ] for s in dsts]))
+                sent += NE_Q // 2
+        if transfers:
+            g.remote_dma_fused(transfers, local_sem=sem.snt)
+        for grp in groups:
+            for (r, a, b) in grp:
+                if b - a == QP:
+                    sent += write(cores[r], T.qs[:, :], T.qs[:, :], sem.qa, NE_Q)
 
-    if core in order:
-        blocks = [(r, b) for r in order[core] for b in range(KB)]
+    if dest[rank] is not None:
+        to, n = (via[rank], NE_ON) if rank in via else (dest[rank], NE_KV)
+        g.wait_ge(ka, 16)
+        sent += write(to, kcols(rank), kcols(rank), ka, n)
+        g.wait_ge(va, 16)
+        sent += write(to, vcols(rank), vcols(rank), va, n)
+
+    if core in work:
+        slots, c0, c1 = work[core]
+        w = c1 - c0
+        blocks = [(r, b) for r in slots for b in range(KB)]
         nb = len(blocks)
         ve.memset(T.zero[:, :], 0.0).then_inc(sem.z, 1)
         ve.wait_ge(sem.z, 1)
-        pe.wait_ge(sem.qa, 16 if core == root else NE_Q)
+        pe.wait_ge(sem.qa, 16 if core == root else (NE_Q if w == QP else NE_Q // 2))
         seen = set()
 
         def arrived(name, r):
-            if cores[r] != core and not SPLIT:
-                name = "ka"
             if (name, r) not in seen:
                 seen.add((name, r))
                 pe.wait_ge(sem["%s%d" % (name, r)], 16 if cores[r] == core else NE_KV)
@@ -164,18 +192,18 @@ def rank_program(g, core, T, topo):
             r, b = blocks[i]
             arrived("ka", r)
             bank = T["ps%d" % (i % NBANK)]
-            pe.matmul(out=bank[:, 0:QP], lhsT=T.kv[:, r * SLOT + b * BW:r * SLOT + (b + 1) * BW], rhs=T.qs[:, :],
+            pe.matmul(out=bank[:, 0:w], lhsT=T.kv[:, r * SLOT + b * BW:r * SLOT + (b + 1) * BW], rhs=T.qs[:, c0:c1],
                       start=True, stop=True).then_inc(sem["sd%d_%d" % (r, b)], 1)
             ve.wait_ge(sem["sd%d_%d" % (r, b)], 1)
-            ve.tensor_tensor(out=T.s[:, (r * KB + b) * QP:(r * KB + b + 1) * QP], in0=bank[:, 0:QP], in1=T.zero[:, :],
+            ve.tensor_tensor(out=T.s[:, (r * KB + b) * QP:(r * KB + b) * QP + w], in0=bank[:, 0:w], in1=T.zero[:, 0:w],
                              op=AluOpType.max).then_inc(sem["rd%d_%d" % (r, b)], 1)
 
         def o_stage(i):
             r, b = blocks[i]
             arrived("va", r)
             pe.wait_ge(sem["rd%d_%d" % (r, b)], 1)
-            pe.matmul(out=T.po[:, 0:QP], lhsT=T.kv[:, r * SLOT + KW + b * BW:r * SLOT + KW + (b + 1) * BW],
-                      rhs=T.s[:, (r * KB + b) * QP:(r * KB + b + 1) * QP],
+            pe.matmul(out=T.po[:, 0:w], lhsT=T.kv[:, r * SLOT + KW + b * BW:r * SLOT + KW + (b + 1) * BW],
+                      rhs=T.s[:, (r * KB + b) * QP:(r * KB + b) * QP + w],
                       start=(i == 0), stop=(i == nb - 1)).then_inc(sem.od, 1)
 
         for i in range(nb + LOOK):
@@ -185,24 +213,26 @@ def rank_program(g, core, T, topo):
                 o_stage(i - LOOK)
 
         if core != root:
+            lead = [grp[0][0] for grp in groups if rank in [x[0] for x in grp]][0]
             ve.wait_ge(sem.od, nb)
-            ve.tensor_copy(out=T.osend[:, :], in_=T.po[:, 0:QP]).then_inc(sem.oc, 1)
+            ve.tensor_copy(out=T.osend[:, 0:w], in_=T.po[:, 0:w]).then_inc(sem.oc, 1)
             g.wait_ge(sem.oc, 1)
-            sent += write(root, T.oin[:, rank * QP:(rank + 1) * QP], T.osend[:, :], sem["oa%d" % rank], NE_O)
+            sent += write(root, T.oin[:, lead * QP + c0:lead * QP + c1], T.osend[:, 0:w], sem["oa%d" % rank], NE_O)
         else:
-            others = [T.rank_of(s) for s in order if s != root]
             ve.wait_ge(sem.od, nb)
             cur = T.po[:, 0:QP]
-            if not others:
+            if not groups:
                 ve.tensor_copy(out=T.ysb[:, :], in_=cur).then_inc(sem.yr, 1)
-            for j, r in enumerate(others):
-                last = j == len(others) - 1
-                ve.wait_ge(sem["oa%d" % r], NE_O)
+            for j, grp in enumerate(groups):
+                last = j == len(groups) - 1
+                lead = grp[0][0]
+                for (r, a, b) in grp:
+                    ve.wait_ge(sem["oa%d" % r], NE_O)
                 out = T.ysb[:, :] if last else T["acc%d" % (j % 2)][:, :]
-                ve.tensor_tensor(out=out, in0=cur, in1=T.oin[:, r * QP:(r + 1) * QP],
-                                 op=AluOpType.add).then_inc(sem.yr if last else sem["ac%d" % r], 1)
+                ve.tensor_tensor(out=out, in0=cur, in1=T.oin[:, lead * QP:(lead + 1) * QP],
+                                 op=AluOpType.add).then_inc(sem.yr if last else sem["ac%d" % lead], 1)
                 if not last:
-                    ve.wait_ge(sem["ac%d" % r], 1)
+                    ve.wait_ge(sem["ac%d" % lead], 1)
                 cur = out
             g.sync.wait_ge(sem.yr, 1)
             g.sync.dma_start(T.y[:, :], T.ysb[:, :]).then_inc(sem.ys, 16)

import numpy as np
from concourse.bass import DstId, RemoteDMATransfer
from concourse.mybir import AluOpType

NR = 12
NCORES = 128
QP = 256
HQ = QP // 2
KB = 2
BW = 128
KW = KB * BW
SLOT = 2 * KW
NBANK = 6
MOVE = 1
PAIRS = 1
VIA_ROOT = 2
VIA_SECOND = 1
LOOK = 2
NE_KV = 8
NE_ON = 8
NE_Q = 8
NE_O = 8

SCRATCH = {
    "qs": ("sbuf", [128, QP], "bfloat16"),
    "kv": ("sbuf", [128, NR * SLOT], "bfloat16"),
    "s": ("sbuf", [128, NR * KB * QP], "bfloat16"),
    "zero": ("sbuf", [128, QP], "float32"),
    "osend": ("sbuf", [128, QP], "bfloat16"),
    "oin": ("sbuf", [128, NR * QP], "bfloat16"),
    "acc0": ("sbuf", [128, QP], "float32"),
    "acc1": ("sbuf", [128, QP], "float32"),
    "ysb": ("sbuf", [128, QP], "bfloat16"),
    "po": ("psum", [128, 512], "float32"),
}
for _i in range(NBANK):
    SCRATCH["ps%d" % _i] = ("psum", [128, 512], "float32")

SEMAPHORES = ["qa", "z", "od", "oc", "yr", "ys", "snt"]
for _r in range(NR):
    SEMAPHORES += ["ka%d" % _r, "va%d" % _r, "oa%d" % _r, "ac%d" % _r]
    for _b in range(KB):
        SEMAPHORES += ["sd%d_%d" % (_r, _b), "rd%d_%d" % (_r, _b)]


def engines(mask, n):
    out, left = 0, n
    for b in range(16):
        if left and (mask >> b) & 1:
            out |= 1 << b
            left -= 1
    return out


def make_plan(T, topo):
    cores = list(T.cores)
    root = cores[T.root]
    chips = [topo.chip(c) for c in cores]
    rchip = topo.chip(root)
    second = None
    for c in cores:
        if topo.mates(topo.chip(c), rchip) and topo.may_write(c, root) and topo.may_write(root, c):
            second = c
    dest, via, work, groups = {}, {}, {}, []
    for r, c in enumerate(cores):
        if len(groups) < PAIRS and c != root and topo.same_plane(chips[r], rchip):
            for m, d in enumerate(cores):
                if topo.mates(chips[m], chips[r]) and topo.may_write(d, c) and topo.may_write(c, d) \
                        and topo.may_write(d, root) and topo.may_write(root, d):
                    dest[r], dest[m] = d, c
                    work[c], work[d] = ([r, m], 0, HQ), ([m, r], HQ, QP)
                    groups.append([(r, 0, HQ), (m, HQ, QP)])
    rest = [r for r in range(len(cores)) if r not in dest]
    far = [r for r in rest if second is not None and cores[r] != second and topo.same_plane(chips[r], topo.chip(second))]
    far.sort(key=lambda r: sum(1 for ch in chips if topo.mates(ch, chips[r])))
    far = far[MOVE:]
    for r in rest:
        dest[r] = second if r in far else (root if cores[r] != root else None)

    def relay(r):
        for x in range(NCORES):
            if topo.chip(x) == chips[r] and topo.die(x) != topo.die(cores[r]) and T.rank_of(x) is None \
                    and topo.may_write(x, dest[r]):
                return x
        return None

    for site, n in ((root, VIA_ROOT), (second, VIA_SECOND)):
        same = [r for r in rest if dest[r] == site and site is not None and topo.same_plane(chips[r], topo.chip(site))]
        for r in (sorted(same)[-n:] if n else []):
            if relay(r) is not None:
                via[r] = relay(r)

    def hops(r, s):
        a, b = chips[r], topo.chip(s)
        if cores[r] == s:
            return 0
        if a == b or topo.mates(a, b):
            return 1
        return (2 if topo.same_plane(a, b) else 3) + (2 if r in via else 0)

    work[root] = (sorted([r for r in rest if r not in far], key=lambda r: (hops(r, root), r)), 0, QP)
    if far:
        work[second] = (sorted(far, key=lambda r: (hops(r, second), r)), 0, QP)
        groups.append([(cores.index(second), 0, QP)])
    return root, dest, via, work, groups


def rank_program(g, core, T, topo):
    rank = T.rank_of(core)
    root, dest, via, work, groups = make_plan(T, topo)
    cores = list(T.cores)
    sem = T.sem
    pe, ve = g.tensor, g.vector
    sent = 0

    def kcols(r):
        return T.kv[:, r * SLOT:r * SLOT + KW]

    def vcols(r):
        return T.kv[:, r * SLOT + KW:(r + 1) * SLOT]

    def write(dst, out_ap, in_ap, rsem, n):
        rid, pid, _ = topo.addr(dst)
        g.remote_dma(out_ap=out_ap, in_ap=in_ap, remote_sem=rsem, local_sem=sem.snt, pid=pid, routing_id=rid,
                     dma_engine_mask=engines(topo.mask(core, dst), n))
        return n

    if rank is None:
        for r in via:
            if via[r] == core:
                g.wait_ge(sem["ka%d" % r], NE_ON)
                sent += write(dest[r], kcols(r), kcols(r), sem["ka%d" % r], NE_KV)
                g.wait_ge(sem["va%d" % r], NE_ON)
                sent += write(dest[r], vcols(r), vcols(r), sem["va%d" % r], NE_KV)
                g.wait_ge(sem.snt, sent)
        return

    ka, va = sem["ka%d" % rank], sem["va%d" % rank]
    if core == root:
        g.sync.dma_start(T.qs[:, :], T.q[:, :]).then_inc(sem.qa, 16)
        g.scalar.dma_start(kcols(rank), T.k[:, :]).then_inc(ka, 16)
        g.sync.dma_start(vcols(rank), T.v[:, :]).then_inc(va, 16)
    else:
        g.sync.dma_start(kcols(rank), T.k[:, :]).then_inc(ka, 16)
        g.scalar.dma_start(vcols(rank), T.v[:, :]).then_inc(va, 16)

    if core == root:
        g.wait_ge(sem.qa, 16)
        transfers, used = [], 0
        for c0 in (0, HQ):
            dsts = [cores[r] for grp in groups for (r, a, b) in grp if a == c0 and b - a == HQ]
            if dsts:
                mask = topo.mask(core, dsts[0])
                for s in dsts:
                    mask &= topo.mask(core, s)
                mine = engines(mask & ~used, NE_Q // 2)
                used |= mine
                transfers.append(RemoteDMATransfer(
                    dst_ids=[DstId(rid=topo.addr(s)[0], pnc=topo.addr(s)[1]) for s in dsts], dma_engine_mask=mine,
                    remote_sem=sem.qa, srcs=[T.qs[:, c0:c0 + HQ]], dsts=[T.qs[:, c0:c0 + HQ] for s in dsts]))
                sent += NE_Q // 2
        if transfers:
            g.remote_dma_fused(transfers, local_sem=sem.snt)
        for grp in groups:
            for (r, a, b) in grp:
                if b - a == QP:
                    sent += write(cores[r], T.qs[:, :], T.qs[:, :], sem.qa, NE_Q)

    if dest[rank] is not None:
        to, n = (via[rank], NE_ON) if rank in via else (dest[rank], NE_KV)
        g.wait_ge(ka, 16)
        sent += write(to, kcols(rank), kcols(rank), ka, n)
        g.wait_ge(va, 16)
        sent += write(to, vcols(rank), vcols(rank), va, n)

    if core in work:
        slots, c0, c1 = work[core]
        w = c1 - c0
        blocks = [(r, b) for r in slots for b in range(KB)]
        nb = len(blocks)
        ve.memset(T.zero[:, :], 0.0).then_inc(sem.z, 1)
        ve.wait_ge(sem.z, 1)
        pe.wait_ge(sem.qa, 16 if core == root else (NE_Q if w == QP else NE_Q // 2))
        seen = set()

        def arrived(name, r):
            if (name, r) not in seen:
                seen.add((name, r))
                pe.wait_ge(sem["%s%d" % (name, r)], 16 if cores[r] == core else NE_KV)

        def s_stage(i):
            r, b = blocks[i]
            arrived("ka", r)
            bank = T["ps%d" % (i % NBANK)]
            pe.matmul(out=bank[:, 0:w], lhsT=T.kv[:, r * SLOT + b * BW:r * SLOT + (b + 1) * BW], rhs=T.qs[:, c0:c1],
                      start=True, stop=True).then_inc(sem["sd%d_%d" % (r, b)], 1)
            ve.wait_ge(sem["sd%d_%d" % (r, b)], 1)
            ve.tensor_tensor(out=T.s[:, (r * KB + b) * QP:(r * KB + b) * QP + w], in0=bank[:, 0:w], in1=T.zero[:, 0:w],
                             op=AluOpType.max).then_inc(sem["rd%d_%d" % (r, b)], 1)

        def o_stage(i):
            r, b = blocks[i]
            arrived("va", r)
            pe.wait_ge(sem["rd%d_%d" % (r, b)], 1)
            pe.matmul(out=T.po[:, 0:w], lhsT=T.kv[:, r * SLOT + KW + b * BW:r * SLOT + KW + (b + 1) * BW],
                      rhs=T.s[:, (r * KB + b) * QP:(r * KB + b) * QP + w],
                      start=(i == 0), stop=(i == nb - 1)).then_inc(sem.od, 1)

        for i in range(nb + LOOK):
            if i < nb:
                s_stage(i)
            if i >= LOOK:
                o_stage(i - LOOK)

        if core != root:
            lead = [grp[0][0] for grp in groups if rank in [x[0] for x in grp]][0]
            ve.wait_ge(sem.od, nb)
            ve.tensor_copy(out=T.osend[:, 0:w], in_=T.po[:, 0:w]).then_inc(sem.oc, 1)
            g.wait_ge(sem.oc, 1)
            sent += write(root, T.oin[:, lead * QP + c0:lead * QP + c1], T.osend[:, 0:w], sem["oa%d" % rank], NE_O)
        else:
            ve.wait_ge(sem.od, nb)
            cur = T.po[:, 0:QP]
            if not groups:
                ve.tensor_copy(out=T.ysb[:, :], in_=cur).then_inc(sem.yr, 1)
            for j, grp in enumerate(groups):
                last = j == len(groups) - 1
                lead = grp[0][0]
                for (r, a, b) in grp:
                    ve.wait_ge(sem["oa%d" % r], NE_O)
                out = T.ysb[:, :] if last else T["acc%d" % (j % 2)][:, :]
                ve.tensor_tensor(out=out, in0=cur, in1=T.oin[:, lead * QP:(lead + 1) * QP],
                                 op=AluOpType.add).then_inc(sem.yr if last else sem["ac%d" % lead], 1)
                if not last:
                    ve.wait_ge(sem["ac%d" % lead], 1)
                cur = out
            g.sync.wait_ge(sem.yr, 1)
            g.sync.dma_start(T.y[:, :], T.ysb[:, :]).then_inc(sem.ys, 16)
            g.sync.wait_ge(sem.ys, 16)

    if sent:
        g.wait_ge(sem.snt, sent)
